import numpy as np
CORES = [6,14,22,30,38,46,54,62,134,142,150,158,166,174,182,190,262,270,278,286,294,302,310,318,390,398,406,414,422,430,438,446]
N = 32
T = 4
ROUTE = [[[21],[20],[8],[24]],[[22],[6],[0],[25]],[[8],[23],[22],[26]],[[31],[19],[17],[20]],[[29],[23],[4],[5]],[[28],[28],[28],[3]],[[16],[15],[9],[6]],[[24],[22],[3],[28]],[[1],[22],[21],[27]],[[11],[19],[2],[18]],[[9],[27],[18],[29]],[[17],[6],[7],[31]],[[5],[31],[13],[29]],[[5],[31],[8],[23]],[[8],[17],[2],[20]],[[11],[5],[4],[23]],[[26],[2],[6],[31]],[[24],[29],[24],[26]],[[19],[29],[0],[1]],[[2],[20],[19],[1]],[[17],[30],[25],[6]],[[3],[14],[26],[25]],[[29],[9],[3],[13]],[[20],[5],[14],[17]],[[25],[13],[5],[27]],[[15],[0],[15],[30]],[[27],[27],[8],[24]],[[27],[30],[13],[20]],[[31],[17],[29],[27]],[[4],[8],[5],[0]],[[19],[2],[18],[8]],[[3],[13],[9],[18]]]
YW = 7
def setup_inputs(rng):
    return {"x": rng.standard_normal((N, 128, T), dtype=np.float32)}
def reference(x):
    y = np.full((N, 128, YW), np.nan, x.dtype)
    fill = [0] * N
    for r in range(N):
        for t in range(T):
            for e in ROUTE[r][t]:
                y[e][:, fill[e]] = x[r][:, t]
                fill[e] += 1
    return {"y": y}

@@ -1,0 +1,80 @@
+from concourse.bass import DstId, RemoteDMATransfer
+
+SCRATCH = {
+    "stage": ("dram", [4, 128, 1], "float32"),
+    "relay": ("dram", [4, 128, 1], "float32"),
+    "land": ("dram", [7, 128, 1], "float32"),
+}
+SEMAPHORES = ["loaded", "sent", "relayed", "arrived", "stored"]
+
+RELAY_CORE = 2
+
+
+def plan(T, topo):
+    route, cores = T.tables["ROUTE"], T.cores
+    own, first, second, lands = {}, {}, {}, {}
+    fill = [0] * len(cores)
+    for r, s in enumerate(cores):
+        for t, experts in enumerate(route[r]):
+            e = experts[0]
+            d, slot = cores[e], fill[e]
+            fill[e] += 1
+            if d == s:
+                own.setdefault(s, []).append((t, slot))
+                continue
+            lands.setdefault(d, []).append(slot)
+            peer_chip = (3 - topo.host(s)) * 128 + topo.chip(s) * 8
+            if topo.rack(topo.host(s)) == topo.rack(topo.host(d)) or d // 8 == peer_chip // 8:
+                first.setdefault(s, []).append((t, d, "land", slot))
+            else:
+                h = peer_chip + RELAY_CORE
+                k = len(second.setdefault(h, []))
+                first.setdefault(s, []).append((t, h, "relay", k))
+                second[h].append((k, d, slot))
+    return own, first, second, lands
+
+
+def send(g, core, T, topo, items):
+    transfers = []
+    for i, (src, d, dst, sem) in enumerate(items):
+        rid, pid = topo.addr(d, core)
+        transfers.append(RemoteDMATransfer(dst_ids=[DstId(rid=rid, pnc=pid)], dma_engine_mask=1 << i, remote_sem=sem,
+                                           src=src, dst=dst))
+    g.remote_dma_fused(transfers, local_sem=T.sem.sent)
+    return len(items)
+
+
+def rank_program(g, core, T, topo):
+    own, first, second, lands = plan(T, topo)
+
+    if core in second:
+        todo = second[core]
+        g.wait_ge(T.sem.relayed, len(todo))
+        n = send(g, core, T, topo, [(T.relay[k], d, T.land[slot], T.sem.arrived) for k, d, slot in todo])
+        g.wait_ge(T.sem.sent, n)
+        return
+    if T.rank_of(core) is None:
+        return
+
+    out = first.get(core, [])
+    for t, d, buf, index in out:
+        g.dma_start(T.stage[t], T.x[:, t:t + 1], allow_slow_non_contiguous=True).then_inc(T.sem.loaded, 16)
+    n_sent = 0
+    if out:
+        g.wait_ge(T.sem.loaded, 16 * len(out))
+        n_sent = send(g, core, T, topo, [(T.stage[t], d, T[buf][index], T.sem.arrived if buf == "land" else T.sem.relayed)
+                                         for t, d, buf, index in out])
+    n_stored = 0
+    for t, slot in own.get(core, []):
+        g.dma_start(T.y[:, slot:slot + 1], T.x[:, t:t + 1], allow_slow_non_contiguous=True).then_inc(T.sem.stored, 16)
+        n_stored += 1
+    slots = lands.get(core, [])
+    if slots:
+        g.wait_ge(T.sem.arrived, len(slots))
+        for slot in slots:
+            g.dma_start(T.y[:, slot:slot + 1], T.land[slot], allow_slow_non_contiguous=True).then_inc(T.sem.stored, 16)
+            n_stored += 1
+    if n_stored:
+        g.wait_ge(T.sem.stored, 16 * n_stored)
+    if n_sent:
+        g.wait_ge(T.sem.sent, n_sent)

@@ -1,80 +1,104 @@
 from concourse.bass import DstId, RemoteDMATransfer
 
 SCRATCH = {
-    "stage": ("dram", [4, 128, 1], "float32"),
-    "relay": ("dram", [4, 128, 1], "float32"),
-    "land": ("dram", [7, 128, 1], "float32"),
+    "xs": ("sbuf", [128, 4], "float32"),
+    "relay": ("sbuf", [128, 4], "float32"),
+    "land": ("sbuf", [128, 7], "float32"),
 }
-SEMAPHORES = ["loaded", "sent", "relayed", "arrived", "stored"]
+SEMAPHORES = ["loaded", "sent", "relayed", "arrived", "stored", "stored_col"]
 
-RELAY_CORE = 2
+
+def engine_sets(k):
+    n = [1] * k
+    grown = True
+    while grown:
+        grown = False
+        for i in range(k):
+            if sum(n) + n[i] <= 8:
+                n[i] *= 2
+                grown = True
+    n.sort(reverse=True)
+    masks, low = [], 0
+    for e in n:
+        masks.append((((1 << e) - 1) << low, e))
+        low += e
+    return masks
 
 
 def plan(T, topo):
     route, cores = T.tables["ROUTE"], T.cores
-    own, first, second, lands = {}, {}, {}, {}
-    fill = [0] * len(cores)
+    own, first, second, width = {}, {}, {}, {}
     for r, s in enumerate(cores):
+        far = ((3 - topo.host(s)) * 16 + topo.chip(s)) * 8
+        helpers = [c for c in range(far, far + 8) if topo.die(c) != topo.die(s)]
         for t, experts in enumerate(route[r]):
-            e = experts[0]
-            d, slot = cores[e], fill[e]
-            fill[e] += 1
+            d = cores[experts[0]]
+            col = width.get(d, 0)
+            width[d] = col + 1
             if d == s:
-                own.setdefault(s, []).append((t, slot))
-                continue
-            lands.setdefault(d, []).append(slot)
-            peer_chip = (3 - topo.host(s)) * 128 + topo.chip(s) * 8
-            if topo.rack(topo.host(s)) == topo.rack(topo.host(d)) or d // 8 == peer_chip // 8:
-                first.setdefault(s, []).append((t, d, "land", slot))
+                own.setdefault(s, []).append((t, col))
+            elif topo.rack(topo.host(s)) == topo.rack(topo.host(d)) or d // 8 == far // 8:
+                first.setdefault(s, []).append((1, "xs", t, d, "land", col))
             else:
-                h = peer_chip + RELAY_CORE
+                h = min((c for c in helpers if topo.may_write(c, d)),
+                        key=lambda c: (len(second.get(c, [])), topo.may_write(c, c ^ 8), c))
                 k = len(second.setdefault(h, []))
-                first.setdefault(s, []).append((t, h, "relay", k))
-                second[h].append((k, d, slot))
-    return own, first, second, lands
+                first.setdefault(s, []).append((0, "xs", t, h, "relay", k))
+                second[h].append((0, "relay", k, d, "land", col))
+    calls, due = {}, {}
+    for table in (first, second):
+        for c, items in table.items():
+            items = sorted(items)
+            calls[c] = []
+            for (order, sbuf, scol, d, dbuf, dcol), (mask, engines) in zip(items, engine_sets(len(items))):
+                calls[c].append((sbuf, scol, d, dbuf, dcol, mask))
+                due.setdefault(d, {}).setdefault(dbuf, 0)
+                due[d][dbuf] += engines
+    return own, calls, due, width
 
 
-def send(g, core, T, topo, items):
-    transfers = []
-    for i, (src, d, dst, sem) in enumerate(items):
+def send(g, core, T, topo, call):
+    transfers, total = [], 0
+    for sbuf, scol, d, dbuf, dcol, mask in call:
         rid, pid = topo.addr(d, core)
-        transfers.append(RemoteDMATransfer(dst_ids=[DstId(rid=rid, pnc=pid)], dma_engine_mask=1 << i, remote_sem=sem,
-                                           src=src, dst=dst))
+        transfers.append(RemoteDMATransfer(dst_ids=[DstId(rid=rid, pnc=pid)], dma_engine_mask=mask,
+                                           remote_sem=T.sem.arrived if dbuf == "land" else T.sem.relayed,
+                                           src=T[sbuf][:, scol:scol + 1], dst=T[dbuf][:, dcol:dcol + 1]))
+        total += bin(mask).count("1")
     g.remote_dma_fused(transfers, local_sem=T.sem.sent)
-    return len(items)
+    return total
 
 
 def rank_program(g, core, T, topo):
-    own, first, second, lands = plan(T, topo)
+    own, calls, due, width = plan(T, topo)
 
-    if core in second:
-        todo = second[core]
-        g.wait_ge(T.sem.relayed, len(todo))
-        n = send(g, core, T, topo, [(T.relay[k], d, T.land[slot], T.sem.arrived) for k, d, slot in todo])
-        g.wait_ge(T.sem.sent, n)
-        return
     if T.rank_of(core) is None:
+        if core in calls:
+            g.wait_ge(T.sem.relayed, due[core]["relay"])
+            g.wait_ge(T.sem.sent, send(g, core, T, topo, calls[core]))
         return
 
-    out = first.get(core, [])
-    for t, d, buf, index in out:
-        g.dma_start(T.stage[t], T.x[:, t:t + 1], allow_slow_non_contiguous=True).then_inc(T.sem.loaded, 16)
-    n_sent = 0
-    if out:
-        g.wait_ge(T.sem.loaded, 16 * len(out))
-        n_sent = send(g, core, T, topo, [(T.stage[t], d, T[buf][index], T.sem.arrived if buf == "land" else T.sem.relayed)
-                                         for t, d, buf, index in out])
-    n_stored = 0
-    for t, slot in own.get(core, []):
-        g.dma_start(T.y[:, slot:slot + 1], T.x[:, t:t + 1], allow_slow_non_contiguous=True).then_inc(T.sem.stored, 16)
-        n_stored += 1
-    slots = lands.get(core, [])
-    if slots:
-        g.wait_ge(T.sem.arrived, len(slots))
-        for slot in slots:
-            g.dma_start(T.y[:, slot:slot + 1], T.land[slot], allow_slow_non_contiguous=True).then_inc(T.sem.stored, 16)
-            n_stored += 1
-    if n_stored:
-        g.wait_ge(T.sem.stored, 16 * n_stored)
-    if n_sent:
-        g.wait_ge(T.sem.sent, n_sent)
+    g.sync.dma_start(T.xs[:], T.x[:]).then_inc(T.sem.loaded, 16)
+    sent = 0
+    if core in calls:
+        g.wait_ge(T.sem.loaded, 16)
+        sent = send(g, core, T, topo, calls[core])
+    expect = due.get(core, {}).get("land", 0)
+    if core in own:
+        g.scalar.wait_ge(T.sem.loaded, 16)
+        for t, col in own[core]:
+            g.scalar.dma_start(T.land[:, col:col + 1], T.xs[:, t:t + 1]).then_inc(T.sem.arrived, 16)
+            expect += 16
+    elif core not in calls:
+        g.wait_ge(T.sem.loaded, 16)
+    n = width.get(core, 0)
+    if n == 1:
+        g.wait_ge(T.sem.arrived, expect)
+        g.dma_start(T.y[:, 0:1], T.land[:, 0:1], allow_slow_non_contiguous=True).then_inc(T.sem.stored_col, 16)
+        g.wait_ge(T.sem.stored_col, 16)
+    elif n > 1:
+        g.sync.wait_ge(T.sem.arrived, expect)
+        g.sync.dma_start(T.y[:, 0:n], T.land[:, 0:n]).then_inc(T.sem.stored, 16)
+        g.wait_ge(T.sem.stored, 16)
+    if sent:
+        g.wait_ge(T.sem.sent, sent)

from concourse.bass import DstId, RemoteDMATransfer

SCRATCH = {
    "xs": ("sbuf", [128, 4], "float32"),
    "relay": ("sbuf", [128, 4], "float32"),
    "land": ("sbuf", [128, 7], "float32"),
}
SEMAPHORES = ["loaded", "sent", "relayed", "arrived", "stored", "stored_col"]


def engine_sets(k):
    n = [1] * k
    grown = True
    while grown:
        grown = False
        for i in range(k):
            if sum(n) + n[i] <= 8:
                n[i] *= 2
                grown = True
    n.sort(reverse=True)
    masks, low = [], 0
    for e in n:
        masks.append((((1 << e) - 1) << low, e))
        low += e
    return masks


def plan(T, topo):
    route, cores = T.tables["ROUTE"], T.cores
    own, first, second, width = {}, {}, {}, {}
    for r, s in enumerate(cores):
        far = ((3 - topo.host(s)) * 16 + topo.chip(s)) * 8
        helpers = [c for c in range(far, far + 8) if topo.die(c) != topo.die(s)]
        for t, experts in enumerate(route[r]):
            d = cores[experts[0]]
            col = width.get(d, 0)
            width[d] = col + 1
            if d == s:
                own.setdefault(s, []).append((t, col))
            elif topo.rack(topo.host(s)) == topo.rack(topo.host(d)) or d // 8 == far // 8:
                first.setdefault(s, []).append((1, "xs", t, d, "land", col))
            else:
                h = min((c for c in helpers if topo.may_write(c, d)),
                        key=lambda c: (len(second.get(c, [])), topo.may_write(c, c ^ 8), c))
                k = len(second.setdefault(h, []))
                first.setdefault(s, []).append((0, "xs", t, h, "relay", k))
                second[h].append((0, "relay", k, d, "land", col))
    calls, due = {}, {}
    for table in (first, second):
        for c, items in table.items():
            items = sorted(items)
            calls[c] = []
            for (order, sbuf, scol, d, dbuf, dcol), (mask, engines) in zip(items, engine_sets(len(items))):
                calls[c].append((sbuf, scol, d, dbuf, dcol, mask))
                due.setdefault(d, {}).setdefault(dbuf, 0)
                due[d][dbuf] += engines
    return own, calls, due, width


def send(g, core, T, topo, call):
    transfers, total = [], 0
    for sbuf, scol, d, dbuf, dcol, mask in call:
        rid, pid = topo.addr(d, core)
        transfers.append(RemoteDMATransfer(dst_ids=[DstId(rid=rid, pnc=pid)], dma_engine_mask=mask,
                                           remote_sem=T.sem.arrived if dbuf == "land" else T.sem.relayed,
                                           src=T[sbuf][:, scol:scol + 1], dst=T[dbuf][:, dcol:dcol + 1]))
        total += bin(mask).count("1")
    g.remote_dma_fused(transfers, local_sem=T.sem.sent)
    return total


def rank_program(g, core, T, topo):
    own, calls, due, width = plan(T, topo)

    if T.rank_of(core) is None:
        if core in calls:
            g.wait_ge(T.sem.relayed, due[core]["relay"])
            g.wait_ge(T.sem.sent, send(g, core, T, topo, calls[core]))
        return

    g.sync.dma_start(T.xs[:], T.x[:]).then_inc(T.sem.loaded, 16)
    sent = 0
    if core in calls:
        g.wait_ge(T.sem.loaded, 16)
        sent = send(g, core, T, topo, calls[core])
    expect = due.get(core, {}).get("land", 0)
    if core in own:
        g.scalar.wait_ge(T.sem.loaded, 16)
        for t, col in own[core]:
            g.scalar.dma_start(T.land[:, col:col + 1], T.xs[:, t:t + 1]).then_inc(T.sem.arrived, 16)
            expect += 16
    elif core not in calls:
        g.wait_ge(T.sem.loaded, 16)
    n = width.get(core, 0)
    if n == 1:
        g.wait_ge(T.sem.arrived, expect)
        g.dma_start(T.y[:, 0:1], T.land[:, 0:1], allow_slow_non_contiguous=True).then_inc(T.sem.stored_col, 16)
        g.wait_ge(T.sem.stored_col, 16)
    elif n > 1:
        g.sync.wait_ge(T.sem.arrived, expect)
        g.sync.dma_start(T.y[:, 0:n], T.land[:, 0:n]).then_inc(T.sem.stored, 16)
        g.wait_ge(T.sem.stored, 16)
    if sent:
        g.wait_ge(T.sem.sent, sent)
